import numpy as np
import ml_dtypes


def mxq(x, axis, fmt="e4m3"):
    dtype, down = {"e4m3": (ml_dtypes.float8_e4m3fn, 7), "e5m2": (ml_dtypes.float8_e5m2, 14)}[fmt]
    v = np.moveaxis(np.asarray(x, np.float32).astype(ml_dtypes.bfloat16).astype(np.float64), axis, -1)
    blocks = v.reshape(v.shape[:-1] + (-1, 32))
    amax = np.abs(blocks).max(-1, keepdims=True)
    byte = np.maximum(np.where(amax > 0, np.frexp(amax)[1] - 1 + 127, 0) - down, 1)
    scale = np.exp2(byte - 127.0)
    codes = (blocks / scale).astype(np.float32).astype(dtype).astype(np.float64)
    return np.moveaxis((codes * scale).reshape(v.shape), -1, axis)


WIDE = False


def mx_kscale(k):
    if not WIDE:
        return np.ones(k)
    levels = np.array([10, -10, 5, -5, 0])
    if k % 512:
        return np.exp2(np.random.permutation(np.resize(levels, k // 32))).repeat(32)
    a = np.empty((k // 512, 16))
    for p in range(k // 512):
        a[p, :8] = np.random.permutation(np.resize(levels, 8))
        for g in range(8):
            far = levels[np.abs(levels - a[p, g]) >= 10]
            a[p, g + 8] = far[np.random.randint(len(far))]
    return np.exp2(a.ravel()).repeat(32)


def f64(x):
    return np.asarray(x).astype(np.float64)


def striped(idx):
    return np.tile(idx.reshape(-1, 16).T, (8, 1)).astype(np.uint16)


def unstriped(offs):
    return offs[:16].T.reshape(-1).astype(np.int64)


def relu(v):
    return np.maximum(v, 0.0)


K, T, S, N = 512, 2048, 512, 128
P = 2 ** 7


def setup_inputs():
    n = np.random.standard_normal
    s = mx_kscale(K)[:, None]
    return {
        "xT": (n((K, T)) * s).astype(np.float32),
        "gate": np.tile(np.random.uniform(0.2, 1.0, S), (P, 1)).astype(np.float32),
        "res": n((N, T)).astype(np.float32),
        "w1": (n((K, N)) / np.sqrt(K) / s).astype(np.float32),
        "offs": striped(np.random.permutation(T)[:S]),
    }


def reference(xT, gate, res, w1, offs):
    r = f64(res)[:, unstriped(offs)]
    xq = mxq(f64(xT)[:, unstriped(offs)], 0, "e4m3")
    y = relu(mxq(f64(w1), 0, "e4m3").T @ xq)
    out = f64(res).copy()
    out[:, unstriped(offs)] = r + y * f64(gate)[:1]
    return out

@@ -1,0 +1,91 @@
+from contextlib import ExitStack
+
+import concourse.mybir as mybir
+
+K, T, S, N = 512, 2048, 512, 128
+FLOPS = 2 * K * S * N
+
+F32 = mybir.dt.float32
+BF16 = mybir.dt.bfloat16
+U32 = mybir.dt.uint32
+U16 = mybir.dt.uint16
+U8 = mybir.dt.uint8
+FP8X4 = mybir.dt.float8_e4m3fn_x4
+ALU = mybir.AluOpType
+
+P = 128
+PACK = 4
+HALVES = 2
+H = S // HALVES
+HC = H // 16
+
+
+def tile_picked_modres_linrelu_l_kernel(tc, xT, gate, res, w1, offs, out):
+    nc = tc.nc
+    with ExitStack() as ctx:
+        pool = ctx.enter_context(tc.tile_pool(name="held", bufs=1))
+        psum = ctx.enter_context(tc.psum_pool(name="psum", bufs=1))
+
+        offsets = pool.tile([P, S // 16], U16, name="offsets")
+        rows = [pool.tile([P, T], F32, name=f"rows{j}") for j in range(PACK)]
+        w_raw = pool.tile([P, PACK, N], F32, name="w_raw")
+        gate_sb = pool.tile([P, S], F32, name="gate_sb")
+        window = pool.tile([P, T], F32, name="window")
+
+        x_rows = xT.rearrange("(p j) t -> j p t", j=PACK)
+        nc.sync.dma_start(rows[0][:], x_rows[0])
+        nc.sync.dma_start(offsets[:], offs)
+        for j in range(1, PACK):
+            nc.sync.dma_start(rows[j][:], x_rows[j])
+        nc.sync.dma_start(w_raw[:], w1.rearrange("(p j) m -> p j m", j=PACK))
+        nc.sync.dma_start(gate_sb[:], gate)
+        nc.sync.dma_start(window[:], res)
+
+        piece = [offsets[:, h * HC : (h + 1) * HC] for h in range(HALVES)]
+        picked = [pool.tile([P, H, PACK], BF16, name=f"picked{h}", align_bytes=64) for h in range(HALVES)]
+        x_codes = [pool.tile([P, H], U32, name=f"x_codes{h}", align_bytes=64) for h in range(HALVES)]
+        x_scales = [pool.tile([P, H], U8, name=f"x_scales{h}", align_bytes=64) for h in range(HALVES)]
+        w_grouped = pool.tile([P, N, PACK], BF16, name="w_grouped", align_bytes=64)
+        w_codes = pool.tile([P, N], U32, name="w_codes", align_bytes=64)
+        w_scales = pool.tile([P, N], U8, name="w_scales", align_bytes=64)
+
+        for j in range(PACK):
+            for h in range(HALVES):
+                nc.vector.tensor_copy(picked[h][:, :, j], rows[j][:].indirect(piece[h]))
+        nc.scalar.copy(w_grouped[:], w_raw[:].rearrange("p j m -> p m j"))
+        for h in range(HALVES):
+            nc.vector.quantize_mx(
+                out=x_codes[h][:].bitcast(FP8X4),
+                scales=x_scales[h][:],
+                in_=picked[h][:].rearrange("p s j -> p (s j)"),
+            )
+        nc.vector.quantize_mx(
+            out=w_codes[:].bitcast(FP8X4),
+            scales=w_scales[:],
+            in_=w_grouped[:].rearrange("p m j -> p (m j)"),
+        )
+
+        gated = [pool.tile([P, H], F32, name=f"gated{h}") for h in range(HALVES)]
+        for h in range(HALVES):
+            acc = psum.tile([P, H], F32, name=f"acc{h}")
+            nc.tensor.matmul_mx(
+                out=acc[:],
+                lhsT=w_codes[:].bitcast(FP8X4),
+                lhsT_scale=w_scales[:],
+                rhs=x_codes[h][:].bitcast(FP8X4),
+                rhs_scale=x_scales[h][:],
+                start=True,
+                stop=True,
+            )
+            nc.vector.scalar_tensor_tensor(
+                gated[h][:], acc[:], 0.0, gate_sb[:, h * H : (h + 1) * H], ALU.max, ALU.mult
+            )
+
+        old = pool.tile([P, S], F32, name="old")
+        new = pool.tile([P, S], F32, name="new")
+        nc.vector.tensor_copy(old[:], window[:].indirect(offsets[:]))
+        for h in range(HALVES):
+            cols = slice(h * H, (h + 1) * H)
+            nc.vector.tensor_tensor(new[:, cols], old[:, cols], gated[h][:], ALU.add)
+        nc.vector.tensor_copy(window[:].indirect(offsets[:]), new[:])
+        nc.sync.dma_start(out, window[:])

@@ -38,8 +38,8 @@ def tile_picked_modres_linrelu_l_kernel(tc, xT, gate, res, w1, offs, out):
         for j in range(1, PACK):
             nc.sync.dma_start(rows[j][:], x_rows[j])
         nc.sync.dma_start(w_raw[:], w1.rearrange("(p j) m -> p j m", j=PACK))
-        nc.sync.dma_start(gate_sb[:], gate)
         nc.sync.dma_start(window[:], res)
+        nc.sync.dma_start(gate_sb[:], gate)
 
         piece = [offsets[:, h * HC : (h + 1) * HC] for h in range(HALVES)]
         picked = [pool.tile([P, H, PACK], BF16, name=f"picked{h}", align_bytes=64) for h in range(HALVES)]
@@ -49,23 +49,32 @@ def tile_picked_modres_linrelu_l_kernel(tc, xT, gate, res, w1, offs, out):
         w_codes = pool.tile([P, N], U32, name="w_codes", align_bytes=64)
         w_scales = pool.tile([P, N], U8, name="w_scales", align_bytes=64)
 
-        for j in range(PACK):
-            for h in range(HALVES):
-                nc.vector.tensor_copy(picked[h][:, :, j], rows[j][:].indirect(piece[h]))
-        nc.scalar.copy(w_grouped[:], w_raw[:].rearrange("p j m -> p m j"))
-        for h in range(HALVES):
+        def quantize(codes, scales, grouped):
             nc.vector.quantize_mx(
-                out=x_codes[h][:].bitcast(FP8X4),
-                scales=x_scales[h][:],
-                in_=picked[h][:].rearrange("p s j -> p (s j)"),
+                out=codes[:].bitcast(FP8X4), scales=scales[:], in_=grouped[:].rearrange("p s j -> p (s j)")
             )
-        nc.vector.quantize_mx(
-            out=w_codes[:].bitcast(FP8X4),
-            scales=w_scales[:],
-            in_=w_grouped[:].rearrange("p m j -> p (m j)"),
-        )
 
-        gated = [pool.tile([P, H], F32, name=f"gated{h}") for h in range(HALVES)]
+        lay = [nc.scalar.copy, nc.vector.tensor_copy]
+        for u in range(2):
+            pair = [pool.tile([P, 2, H], F32, name=f"pair{u}_{h}") for h in range(HALVES)]
+            for e in range(2):
+                for h in range(HALVES):
+                    nc.vector.tensor_copy(pair[h][:, e, :], rows[2 * u + e][:].indirect(piece[h]))
+            for h in range(HALVES):
+                lay[h](picked[h][:, :, 2 * u : 2 * u + 2], pair[h][:].rearrange("p e s -> p s e"))
+        nc.scalar.copy(
+            w_grouped[:].rearrange("p (c i) j -> p c j i", i=4),
+            w_raw[:].rearrange("p j (c i) -> p c j i", i=4),
+        )
+        quantize(x_codes[0], x_scales[0], picked[0])
+        quantize(x_codes[1], x_scales[1], picked[1])
+        quantize(w_codes, w_scales, w_grouped)
+
+        old = pool.tile([P, S], F32, name="old")
+        gated = pool.tile([P, S], F32, name="gated")
+        new = pool.tile([P, S], F32, name="new")
+        half = [slice(h * H, (h + 1) * H) for h in range(HALVES)]
+        nc.vector.tensor_copy(old[:], window[:].indirect(offsets[:]))
         for h in range(HALVES):
             acc = psum.tile([P, H], F32, name=f"acc{h}")
             nc.tensor.matmul_mx(
@@ -77,15 +86,8 @@ def tile_picked_modres_linrelu_l_kernel(tc, xT, gate, res, w1, offs, out):
                 start=True,
                 stop=True,
             )
-            nc.vector.scalar_tensor_tensor(
-                gated[h][:], acc[:], 0.0, gate_sb[:, h * H : (h + 1) * H], ALU.max, ALU.mult
-            )
-
-        old = pool.tile([P, S], F32, name="old")
-        new = pool.tile([P, S], F32, name="new")
-        nc.vector.tensor_copy(old[:], window[:].indirect(offsets[:]))
+            nc.vector.scalar_tensor_tensor(gated[:, half[h]], acc[:], 0.0, gate_sb[:, half[h]], ALU.max, ALU.mult)
         for h in range(HALVES):
-            cols = slice(h * H, (h + 1) * H)
-            nc.vector.tensor_tensor(new[:, cols], old[:, cols], gated[h][:], ALU.add)
+            nc.vector.tensor_tensor(new[:, half[h]], old[:, half[h]], gated[:, half[h]], ALU.add)
         nc.vector.tensor_copy(window[:].indirect(offsets[:]), new[:])
         nc.sync.dma_start(out, window[:])

@@ -27,16 +27,18 @@ def tile_picked_modres_linrelu_l_kernel(tc, xT, gate, res, w1, offs, out):
         psum = ctx.enter_context(tc.psum_pool(name="psum", bufs=1))
 
         offsets = pool.tile([P, S // 16], U16, name="offsets")
-        rows = [pool.tile([P, T], F32, name=f"rows{j}") for j in range(PACK)]
+        first = pool.tile([P, 2, T], F32, name="first")
+        later = [pool.tile([P, T], F32, name=f"later{j}") for j in range(2)]
+        rows = [first[:, 0, :], first[:, 1, :], later[0][:], later[1][:]]
         w_raw = pool.tile([P, PACK, N], F32, name="w_raw")
         gate_sb = pool.tile([P, S], F32, name="gate_sb")
         window = pool.tile([P, T], F32, name="window")
 
-        x_rows = xT.rearrange("(p j) t -> j p t", j=PACK)
-        nc.sync.dma_start(rows[0][:], x_rows[0])
+        x_rows = xT.rearrange("(p j) t -> p j t", j=PACK)
+        nc.sync.dma_start(first[:], x_rows[:, 0:2, :])
         nc.sync.dma_start(offsets[:], offs)
-        for j in range(1, PACK):
-            nc.sync.dma_start(rows[j][:], x_rows[j])
+        nc.sync.dma_start(later[0][:], x_rows[:, 2, :])
+        nc.sync.dma_start(later[1][:], x_rows[:, 3, :])
         nc.sync.dma_start(w_raw[:], w1.rearrange("(p j) m -> p j m", j=PACK))
         nc.sync.dma_start(window[:], res)
         nc.sync.dma_start(gate_sb[:], gate)
@@ -54,21 +56,27 @@ def tile_picked_modres_linrelu_l_kernel(tc, xT, gate, res, w1, offs, out):
                 out=codes[:].bitcast(FP8X4), scales=scales[:], in_=grouped[:].rearrange("p s j -> p (s j)")
             )
 
-        lay = [nc.scalar.copy, nc.vector.tensor_copy]
-        for u in range(2):
-            pair = [pool.tile([P, 2, H], F32, name=f"pair{u}_{h}") for h in range(HALVES)]
-            for e in range(2):
-                for h in range(HALVES):
-                    nc.vector.tensor_copy(pair[h][:, e, :], rows[2 * u + e][:].indirect(piece[h]))
+        Q = H // 2
+
+        def lay(copy, h, u, tokens):
+            copy(picked[h][:, tokens, 2 * u : 2 * u + 2], pair[u][h][:, :, tokens].rearrange("p e s -> p s e"))
+
+        pair = [[pool.tile([P, 2, H], F32, name=f"pair{u}_{h}") for h in range(HALVES)] for u in range(2)]
+        for j in range(PACK):
             for h in range(HALVES):
-                lay[h](picked[h][:, :, 2 * u : 2 * u + 2], pair[h][:].rearrange("p e s -> p s e"))
+                nc.vector.tensor_copy(pair[j // 2][h][:, j % 2, :], rows[j].indirect(piece[h]))
+        for h in range(HALVES):
+            lay(nc.scalar.copy, h, 0, slice(0, H))
+        lay(nc.scalar.copy, 0, 1, slice(0, Q))
+        lay(nc.vector.tensor_copy, 0, 1, slice(Q, H))
+        lay(nc.vector.tensor_copy, 1, 1, slice(0, H))
         nc.scalar.copy(
             w_grouped[:].rearrange("p (c i) j -> p c j i", i=4),
             w_raw[:].rearrange("p j (c i) -> p c j i", i=4),
         )
         quantize(x_codes[0], x_scales[0], picked[0])
-        quantize(x_codes[1], x_scales[1], picked[1])
         quantize(w_codes, w_scales, w_grouped)
+        quantize(x_codes[1], x_scales[1], picked[1])
 
         old = pool.tile([P, S], F32, name="old")
         gated = pool.tile([P, S], F32, name="gated")

@@ -80,7 +80,6 @@ def tile_picked_modres_linrelu_l_kernel(tc, xT, gate, res, w1, offs, out):
 
         old = pool.tile([P, S], F32, name="old")
         gated = pool.tile([P, S], F32, name="gated")
-        new = pool.tile([P, S], F32, name="new")
         half = [slice(h * H, (h + 1) * H) for h in range(HALVES)]
         nc.vector.tensor_copy(old[:], window[:].indirect(offsets[:]))
         for h in range(HALVES):
@@ -95,7 +94,5 @@ def tile_picked_modres_linrelu_l_kernel(tc, xT, gate, res, w1, offs, out):
                 stop=True,
             )
             nc.vector.scalar_tensor_tensor(gated[:, half[h]], acc[:], 0.0, gate_sb[:, half[h]], ALU.max, ALU.mult)
-        for h in range(HALVES):
-            nc.vector.tensor_tensor(new[:, half[h]], old[:, half[h]], gated[:, half[h]], ALU.add)
-        nc.vector.tensor_copy(window[:].indirect(offsets[:]), new[:])
+        nc.vector.tensor_tensor(window[:].indirect(offsets[:]), old[:], gated[:], ALU.add)
         nc.sync.dma_start(out, window[:])

@@ -12,11 +12,12 @@ U16 = mybir.dt.uint16
 U8 = mybir.dt.uint8
 FP8X4 = mybir.dt.float8_e4m3fn_x4
 ALU = mybir.AluOpType
+ACT = mybir.ActivationFunctionType
 
 P = 128
 PACK = 4
-HALVES = 2
-H = S // HALVES
+PIECES = 4
+H = S // PIECES
 HC = H // 16
 
 
@@ -29,7 +30,6 @@ def tile_picked_modres_linrelu_l_kernel(tc, xT, gate, res, w1, offs, out):
         offsets = pool.tile([P, S // 16], U16, name="offsets")
         first = pool.tile([P, 2, T], F32, name="first")
         later = [pool.tile([P, T], F32, name=f"later{j}") for j in range(2)]
-        rows = [first[:, 0, :], first[:, 1, :], later[0][:], later[1][:]]
         w_raw = pool.tile([P, PACK, N], F32, name="w_raw")
         gate_sb = pool.tile([P, S], F32, name="gate_sb")
         window = pool.tile([P, T], F32, name="window")
@@ -43,56 +43,59 @@ def tile_picked_modres_linrelu_l_kernel(tc, xT, gate, res, w1, offs, out):
         nc.sync.dma_start(window[:], res)
         nc.sync.dma_start(gate_sb[:], gate)
 
-        piece = [offsets[:, h * HC : (h + 1) * HC] for h in range(HALVES)]
-        picked = [pool.tile([P, H, PACK], BF16, name=f"picked{h}", align_bytes=64) for h in range(HALVES)]
-        x_codes = [pool.tile([P, H], U32, name=f"x_codes{h}", align_bytes=64) for h in range(HALVES)]
-        x_scales = [pool.tile([P, H], U8, name=f"x_scales{h}", align_bytes=64) for h in range(HALVES)]
+        piece = [offsets[:, h * HC : (h + 1) * HC] for h in range(PIECES)]
+        span = [slice(h * H, (h + 1) * H) for h in range(PIECES)]
+        picked = [pool.tile([P, H, PACK], BF16, name=f"picked{h}", align_bytes=64) for h in range(PIECES)]
+        x_codes = [pool.tile([P, S // 2], U32, name=f"x_codes{g}", align_bytes=64) for g in range(2)]
+        x_scales = [pool.tile([P, S // 2], U8, name=f"x_scales{g}", align_bytes=64) for g in range(2)]
         w_grouped = pool.tile([P, N, PACK], BF16, name="w_grouped", align_bytes=64)
         w_codes = pool.tile([P, N], U32, name="w_codes", align_bytes=64)
         w_scales = pool.tile([P, N], U8, name="w_scales", align_bytes=64)
 
         def quantize(codes, scales, grouped):
-            nc.vector.quantize_mx(
-                out=codes[:].bitcast(FP8X4), scales=scales[:], in_=grouped[:].rearrange("p s j -> p (s j)")
-            )
+            nc.vector.quantize_mx(out=codes.bitcast(FP8X4), scales=scales, in_=grouped[:].rearrange("p s j -> p (s j)"))
 
-        Q = H // 2
+        early = pool.tile([P, 2, S], F32, name="early")
+        late = [pool.tile([P, 2, H], BF16, name=f"late{h}") for h in range(PIECES)]
+        for j in range(2):
+            nc.vector.tensor_copy(early[:, j, :], first[:, j, :].indirect(offsets[:]))
+        for h in range(PIECES):
+            nc.scalar.copy(picked[h][:, :, 0:2], early[:, :, span[h]].rearrange("p e s -> p s e"))
+        for j in range(2):
+            for h in range(PIECES):
+                nc.vector.tensor_copy(late[h][:, j, :], later[j][:].indirect(piece[h]))
 
-        def lay(copy, h, u, tokens):
-            copy(picked[h][:, tokens, 2 * u : 2 * u + 2], pair[u][h][:, :, tokens].rearrange("p e s -> p s e"))
+        def lay(copy, h):
+            copy(picked[h][:, :, 2:4], late[h][:].rearrange("p e s -> p s e"))
 
-        pair = [[pool.tile([P, 2, H], F32, name=f"pair{u}_{h}") for h in range(HALVES)] for u in range(2)]
-        for j in range(PACK):
-            for h in range(HALVES):
-                nc.vector.tensor_copy(pair[j // 2][h][:, j % 2, :], rows[j].indirect(piece[h]))
-        for h in range(HALVES):
-            lay(nc.scalar.copy, h, 0, slice(0, H))
-        lay(nc.scalar.copy, 0, 1, slice(0, Q))
-        lay(nc.vector.tensor_copy, 0, 1, slice(Q, H))
-        lay(nc.vector.tensor_copy, 1, 1, slice(0, H))
-        nc.scalar.copy(
-            w_grouped[:].rearrange("p (c i) j -> p c j i", i=4),
-            w_raw[:].rearrange("p j (c i) -> p c j i", i=4),
-        )
-        quantize(x_codes[0], x_scales[0], picked[0])
-        quantize(w_codes, w_scales, w_grouped)
-        quantize(x_codes[1], x_scales[1], picked[1])
+        def quantize_piece(h):
+            quantize(x_codes[h // 2][:, span[h % 2]], x_scales[h // 2][:, span[h % 2]], picked[h])
+
+        nc.gpsimd.tensor_scalar(w_grouped[:], w_raw[:].rearrange("p j m -> p m j"), 1.0, 0.0, ALU.mult, ALU.add)
+        for h in range(PIECES):
+            lay(nc.scalar.copy, h)
+        quantize(w_codes[:], w_scales[:], w_grouped)
+        for h in range(PIECES):
+            quantize_piece(h)
 
         old = pool.tile([P, S], F32, name="old")
         gated = pool.tile([P, S], F32, name="gated")
-        half = [slice(h * H, (h + 1) * H) for h in range(HALVES)]
-        nc.vector.tensor_copy(old[:], window[:].indirect(offsets[:]))
-        for h in range(HALVES):
-            acc = psum.tile([P, H], F32, name=f"acc{h}")
+        cols = [slice(g * S // 2, (g + 1) * S // 2) for g in range(2)]
+        acc = [psum.tile([P, S // 2], F32, name=f"acc{g}") for g in range(2)]
+        for g in range(2):
             nc.tensor.matmul_mx(
-                out=acc[:],
+                out=acc[g][:],
                 lhsT=w_codes[:].bitcast(FP8X4),
                 lhsT_scale=w_scales[:],
-                rhs=x_codes[h][:].bitcast(FP8X4),
-                rhs_scale=x_scales[h][:],
+                rhs=x_codes[g][:].bitcast(FP8X4),
+                rhs_scale=x_scales[g][:],
                 start=True,
                 stop=True,
             )
-            nc.vector.scalar_tensor_tensor(gated[:, half[h]], acc[:], 0.0, gate_sb[:, half[h]], ALU.max, ALU.mult)
+        rectified = pool.tile([P, S // 2], F32, name="rectified")
+        nc.scalar.activation(rectified[:], acc[0][:], ACT.Relu)
+        nc.gpsimd.tensor_tensor(gated[:, cols[0]], rectified[:], gate_sb[:, cols[0]], ALU.mult)
+        nc.vector.tensor_copy(old[:], window[:].indirect(offsets[:]))
+        nc.vector.scalar_tensor_tensor(gated[:, cols[1]], acc[1][:], 0.0, gate_sb[:, cols[1]], ALU.max, ALU.mult)
         nc.vector.tensor_tensor(window[:].indirect(offsets[:]), old[:], gated[:], ALU.add)
         nc.sync.dma_start(out, window[:])

@@ -1,6 +1,7 @@
 from contextlib import ExitStack
 
 import concourse.mybir as mybir
+from concourse.masks import make_identity
 
 K, T, S, N = 512, 2048, 512, 128
 FLOPS = 2 * K * S * N
@@ -16,9 +17,6 @@ ACT = mybir.ActivationFunctionType
 
 P = 128
 PACK = 4
-PIECES = 4
-H = S // PIECES
-HC = H // 16
 
 
 def tile_picked_modres_linrelu_l_kernel(tc, xT, gate, res, w1, offs, out):
@@ -31,71 +29,89 @@ def tile_picked_modres_linrelu_l_kernel(tc, xT, gate, res, w1, offs, out):
         first = pool.tile([P, 2, T], F32, name="first")
         later = [pool.tile([P, T], F32, name=f"later{j}") for j in range(2)]
         w_raw = pool.tile([P, PACK, N], F32, name="w_raw")
-        gate_sb = pool.tile([P, S], F32, name="gate_sb")
+        gate_dealt = pool.tile([P, PACK], F32, name="gate_dealt")
         window = pool.tile([P, T], F32, name="window")
 
         x_rows = xT.rearrange("(p j) t -> p j t", j=PACK)
         nc.sync.dma_start(first[:], x_rows[:, 0:2, :])
         nc.sync.dma_start(offsets[:], offs)
+        nc.sync.dma_start(gate_dealt[:], gate[0:1, :].rearrange("o (p c) -> (o p) c", c=PACK))
         nc.sync.dma_start(later[0][:], x_rows[:, 2, :])
         nc.sync.dma_start(later[1][:], x_rows[:, 3, :])
         nc.sync.dma_start(w_raw[:], w1.rearrange("(p j) m -> p j m", j=PACK))
         nc.sync.dma_start(window[:], res)
-        nc.sync.dma_start(gate_sb[:], gate)
 
-        piece = [offsets[:, h * HC : (h + 1) * HC] for h in range(PIECES)]
-        span = [slice(h * H, (h + 1) * H) for h in range(PIECES)]
-        picked = [pool.tile([P, H, PACK], BF16, name=f"picked{h}", align_bytes=64) for h in range(PIECES)]
-        x_codes = [pool.tile([P, S // 2], U32, name=f"x_codes{g}", align_bytes=64) for g in range(2)]
-        x_scales = [pool.tile([P, S // 2], U8, name=f"x_scales{g}", align_bytes=64) for g in range(2)]
-        w_grouped = pool.tile([P, N, PACK], BF16, name="w_grouped", align_bytes=64)
-        w_codes = pool.tile([P, N], U32, name="w_codes", align_bytes=64)
-        w_scales = pool.tile([P, N], U8, name="w_scales", align_bytes=64)
+        identity = pool.tile([P, P], F32, name="identity")
+        make_identity(nc, identity[:])
+        gate_ps = psum.tile([P, PACK, P], F32, name="gate_ps")
+        for c in range(PACK):
+            nc.tensor.transpose(gate_ps[:, c, :], gate_dealt[:, c : c + 1].to_broadcast([P, P]), identity[:])
+        gate_sb = pool.tile([P, S], F32, name="gate_sb")
+        nc.scalar.copy(gate_sb[:].rearrange("p (n c) -> p n c", c=PACK), gate_ps[:].rearrange("p c n -> p n c"))
+
+        half = S // 2
+        part = half // 2
+        lists = [offsets[:, g * half // 16 : (g + 1) * half // 16] for g in range(2)]
+        span = [slice(g * half, (g + 1) * half) for g in range(2)]
+        parts = [slice(h * part, (h + 1) * part) for h in range(2)]
+        joint = pool.tile([P, N + half, PACK], BF16, name="joint", align_bytes=64)
+        joint_codes = pool.tile([P, N + half], U32, name="joint_codes", align_bytes=64)
+        joint_scales = pool.tile([P, N + half], U8, name="joint_scales", align_bytes=64)
+        second = pool.tile([P, half, PACK], BF16, name="second", align_bytes=64)
+        picked = [joint[:, N:, :], second[:]]
 
         def quantize(codes, scales, grouped):
-            nc.vector.quantize_mx(out=codes.bitcast(FP8X4), scales=scales, in_=grouped[:].rearrange("p s j -> p (s j)"))
+            nc.vector.quantize_mx(out=codes[:].bitcast(FP8X4), scales=scales[:], in_=grouped.rearrange("p s j -> p (s j)"))
+
+        def scalar_gather(dst, src):
+            nc.scalar.activation(dst, src, ACT.Copy)
 
         early = pool.tile([P, 2, S], F32, name="early")
-        late = [pool.tile([P, 2, H], BF16, name=f"late{h}") for h in range(PIECES)]
+        late = pool.tile([P, 2, half], BF16, name="late")
         for j in range(2):
             nc.vector.tensor_copy(early[:, j, :], first[:, j, :].indirect(offsets[:]))
-        for h in range(PIECES):
-            nc.scalar.copy(picked[h][:, :, 0:2], early[:, :, span[h]].rearrange("p e s -> p s e"))
+        for g, copy in enumerate((nc.vector.tensor_copy, nc.scalar.copy)):
+            copy(picked[g][:, :, 0:2], early[:, :, span[g]].rearrange("p e s -> p s e"))
         for j in range(2):
-            for h in range(PIECES):
-                nc.vector.tensor_copy(late[h][:, j, :], later[j][:].indirect(piece[h]))
+            nc.vector.tensor_copy(picked[0][:, :, 2 + j], later[j][:].indirect(lists[0]))
+            scalar_gather(late[:, j, :], later[j][:].indirect(lists[1]))
+        nc.scalar.copy(picked[1][:, :, 2:4], late[:].rearrange("p e s -> p s e"))
+        nc.vector.tensor_copy(joint[:, 0:N, :], w_raw[:].rearrange("p j m -> p m j"))
 
-        def lay(copy, h):
-            copy(picked[h][:, :, 2:4], late[h][:].rearrange("p e s -> p s e"))
-
-        def quantize_piece(h):
-            quantize(x_codes[h // 2][:, span[h % 2]], x_scales[h // 2][:, span[h % 2]], picked[h])
-
-        nc.gpsimd.tensor_scalar(w_grouped[:], w_raw[:].rearrange("p j m -> p m j"), 1.0, 0.0, ALU.mult, ALU.add)
-        for h in range(PIECES):
-            lay(nc.scalar.copy, h)
-        quantize(w_codes[:], w_scales[:], w_grouped)
-        for h in range(PIECES):
-            quantize_piece(h)
-
-        old = pool.tile([P, S], F32, name="old")
-        gated = pool.tile([P, S], F32, name="gated")
-        cols = [slice(g * S // 2, (g + 1) * S // 2) for g in range(2)]
-        acc = [psum.tile([P, S // 2], F32, name=f"acc{g}") for g in range(2)]
-        for g in range(2):
+        def product(acc, codes, scales):
             nc.tensor.matmul_mx(
-                out=acc[g][:],
-                lhsT=w_codes[:].bitcast(FP8X4),
-                lhsT_scale=w_scales[:],
-                rhs=x_codes[g][:].bitcast(FP8X4),
-                rhs_scale=x_scales[g][:],
+                out=acc[:],
+                lhsT=joint_codes[:, 0:N].bitcast(FP8X4),
+                lhsT_scale=joint_scales[:, 0:N],
+                rhs=codes.bitcast(FP8X4),
+                rhs_scale=scales,
                 start=True,
                 stop=True,
             )
-        rectified = pool.tile([P, S // 2], F32, name="rectified")
-        nc.scalar.activation(rectified[:], acc[0][:], ACT.Relu)
-        nc.gpsimd.tensor_tensor(gated[:, cols[0]], rectified[:], gate_sb[:, cols[0]], ALU.mult)
-        nc.vector.tensor_copy(old[:], window[:].indirect(offsets[:]))
-        nc.vector.scalar_tensor_tensor(gated[:, cols[1]], acc[1][:], 0.0, gate_sb[:, cols[1]], ALU.max, ALU.mult)
-        nc.vector.tensor_tensor(window[:].indirect(offsets[:]), old[:], gated[:], ALU.add)
+
+        def relu_gate(gated, acc, gate_cols):
+            nc.vector.scalar_tensor_tensor(gated, acc[:], 0.0, gate_cols, ALU.max, ALU.mult)
+
+        new = pool.tile([P, half], F32, name="new")
+        old = pool.tile([P, half], F32, name="old")
+        acc0 = [psum.tile([P, part], F32, name=f"acc0{h}") for h in range(2)]
+        gated0 = pool.tile([P, half], F32, name="gated0", tag="turn", align_bytes=64)
+        quantize(joint_codes, joint_scales, joint[:])
+        for h in range(2):
+            cols = slice(N + h * part, N + (h + 1) * part)
+            product(acc0[h], joint_codes[:, cols], joint_scales[:, cols])
+            relu_gate(gated0[:, parts[h]], acc0[h], gate_sb[:, parts[h]])
+        for h in range(2):
+            entries = offsets[:, h * part // 16 : (h + 1) * part // 16]
+            nc.vector.tensor_tensor(new[:, parts[h]], window[:].indirect(entries), gated0[:, parts[h]], ALU.add)
+        scalar_gather(old[:], window[:].indirect(lists[1]))
+        codes1 = pool.tile([P, half], U32, name="codes1", tag="turn", align_bytes=64)
+        scales1 = pool.tile([P, half], U8, name="scales1", align_bytes=64)
+        acc1 = psum.tile([P, half], F32, name="acc1")
+        gated = pool.tile([P, half], F32, name="gated")
+        quantize(codes1, scales1, picked[1])
+        product(acc1, codes1[:], scales1[:])
+        relu_gate(gated[:], acc1, gate_sb[:, span[1]])
+        nc.scalar.activation(window[:].indirect(lists[0]), new[:], ACT.Copy)
+        nc.vector.tensor_tensor(window[:].indirect(lists[1]), old[:], gated[:], ALU.add)
         nc.sync.dma_start(out, window[:])

@@ -1,7 +1,6 @@
 from contextlib import ExitStack
 
 import concourse.mybir as mybir
-from concourse.masks import make_identity
 
 K, T, S, N = 512, 2048, 512, 128
 FLOPS = 2 * K * S * N
@@ -29,36 +28,32 @@ def tile_picked_modres_linrelu_l_kernel(tc, xT, gate, res, w1, offs, out):
         first = pool.tile([P, 2, T], F32, name="first")
         later = [pool.tile([P, T], F32, name=f"later{j}") for j in range(2)]
         w_raw = pool.tile([P, PACK, N], F32, name="w_raw")
-        gate_dealt = pool.tile([P, PACK], F32, name="gate_dealt")
+        gate_sb = pool.tile([P, S], F32, name="gate_sb")
         window = pool.tile([P, T], F32, name="window")
 
         x_rows = xT.rearrange("(p j) t -> p j t", j=PACK)
         nc.sync.dma_start(first[:], x_rows[:, 0:2, :])
         nc.sync.dma_start(offsets[:], offs)
-        nc.sync.dma_start(gate_dealt[:], gate[0:1, :].rearrange("o (p c) -> (o p) c", c=PACK))
         nc.sync.dma_start(later[0][:], x_rows[:, 2, :])
         nc.sync.dma_start(later[1][:], x_rows[:, 3, :])
         nc.sync.dma_start(w_raw[:], w1.rearrange("(p j) m -> p j m", j=PACK))
         nc.sync.dma_start(window[:], res)
-
-        identity = pool.tile([P, P], F32, name="identity")
-        make_identity(nc, identity[:])
-        gate_ps = psum.tile([P, PACK, P], F32, name="gate_ps")
-        for c in range(PACK):
-            nc.tensor.transpose(gate_ps[:, c, :], gate_dealt[:, c : c + 1].to_broadcast([P, P]), identity[:])
-        gate_sb = pool.tile([P, S], F32, name="gate_sb")
-        nc.scalar.copy(gate_sb[:].rearrange("p (n c) -> p n c", c=PACK), gate_ps[:].rearrange("p c n -> p n c"))
+        nc.sync.dma_start(gate_sb[:], gate)
 
         half = S // 2
         part = half // 2
-        lists = [offsets[:, g * half // 16 : (g + 1) * half // 16] for g in range(2)]
-        span = [slice(g * half, (g + 1) * half) for g in range(2)]
-        parts = [slice(h * part, (h + 1) * part) for h in range(2)]
-        joint = pool.tile([P, N + half, PACK], BF16, name="joint", align_bytes=64)
-        joint_codes = pool.tile([P, N + half], U32, name="joint_codes", align_bytes=64)
-        joint_scales = pool.tile([P, N + half], U8, name="joint_scales", align_bytes=64)
-        second = pool.tile([P, half, PACK], BF16, name="second", align_bytes=64)
-        picked = [joint[:, N:, :], second[:]]
+
+        def entries(lo, hi):
+            return offsets[:, lo // 16 : hi // 16]
+
+        stepped = pool.tile([P, half, PACK], BF16, name="stepped", align_bytes=64)
+        laid = [pool.tile([P, part, PACK], BF16, name=f"laid{h}", align_bytes=64) for h in range(2)]
+        codes = [pool.tile([P, part], U32, name=f"codes{h}", align_bytes=64) for h in range(4)]
+        scales = [pool.tile([P, part], U8, name=f"scales{h}", align_bytes=64) for h in range(4)]
+        w_grouped = pool.tile([P, N, PACK], BF16, name="w_grouped", align_bytes=64)
+        w_codes = pool.tile([P, N], U32, name="w_codes", align_bytes=64)
+        w_scales = pool.tile([P, N], U8, name="w_scales", align_bytes=64)
+        span = [slice(h * part, (h + 1) * part) for h in range(4)]
 
         def quantize(codes, scales, grouped):
             nc.vector.quantize_mx(out=codes[:].bitcast(FP8X4), scales=scales[:], in_=grouped.rearrange("p s j -> p (s j)"))
@@ -67,51 +62,43 @@ def tile_picked_modres_linrelu_l_kernel(tc, xT, gate, res, w1, offs, out):
             nc.scalar.activation(dst, src, ACT.Copy)
 
         early = pool.tile([P, 2, S], F32, name="early")
-        late = pool.tile([P, 2, half], BF16, name="late")
+        late = [pool.tile([P, 2, part], BF16, name=f"late{h}") for h in range(2)]
         for j in range(2):
             nc.vector.tensor_copy(early[:, j, :], first[:, j, :].indirect(offsets[:]))
-        for g, copy in enumerate((nc.vector.tensor_copy, nc.scalar.copy)):
-            copy(picked[g][:, :, 0:2], early[:, :, span[g]].rearrange("p e s -> p s e"))
+        nc.vector.tensor_copy(stepped[:, :, 0:2], early[:, :, 0:half].rearrange("p e s -> p s e"))
+        for h in range(2):
+            nc.scalar.copy(laid[h][:, :, 0:2], early[:, :, span[2 + h]].rearrange("p e s -> p s e"))
         for j in range(2):
-            nc.vector.tensor_copy(picked[0][:, :, 2 + j], later[j][:].indirect(lists[0]))
-            scalar_gather(late[:, j, :], later[j][:].indirect(lists[1]))
-        nc.scalar.copy(picked[1][:, :, 2:4], late[:].rearrange("p e s -> p s e"))
-        nc.vector.tensor_copy(joint[:, 0:N, :], w_raw[:].rearrange("p j m -> p m j"))
+            nc.vector.tensor_copy(stepped[:, :, 2 + j], later[j][:].indirect(entries(0, half)))
+            for h in range(2):
+                scalar_gather(late[h][:, j, :], later[j][:].indirect(entries(half + h * part, half + (h + 1) * part)))
+        for h in range(2):
+            nc.scalar.copy(laid[h][:, :, 2:4], late[h][:].rearrange("p e s -> p s e"))
+        nc.gpsimd.tensor_scalar(w_grouped[:], w_raw[:].rearrange("p j m -> p m j"), 1.0, 0.0, ALU.mult, ALU.add)
+        quantize(w_codes, w_scales, w_grouped[:])
+        grouped = [stepped[:, span[0], :], stepped[:, span[1], :], laid[0][:], laid[1][:]]
+        for h in range(4):
+            quantize(codes[h], scales[h], grouped[h])
 
-        def product(acc, codes, scales):
+        acc = [psum.tile([P, part], F32, name="acc0"), psum.tile([P, S - part], F32, name="acc1")]
+        outs = [acc[0][:]] + [acc[1][:, span[h]] for h in range(3)]
+        for h in range(4):
             nc.tensor.matmul_mx(
-                out=acc[:],
-                lhsT=joint_codes[:, 0:N].bitcast(FP8X4),
-                lhsT_scale=joint_scales[:, 0:N],
-                rhs=codes.bitcast(FP8X4),
-                rhs_scale=scales,
+                out=outs[h],
+                lhsT=w_codes[:].bitcast(FP8X4),
+                lhsT_scale=w_scales[:],
+                rhs=codes[h][:].bitcast(FP8X4),
+                rhs_scale=scales[h][:],
                 start=True,
                 stop=True,
             )
-
-        def relu_gate(gated, acc, gate_cols):
-            nc.vector.scalar_tensor_tensor(gated, acc[:], 0.0, gate_cols, ALU.max, ALU.mult)
-
-        new = pool.tile([P, half], F32, name="new")
-        old = pool.tile([P, half], F32, name="old")
-        acc0 = [psum.tile([P, part], F32, name=f"acc0{h}") for h in range(2)]
-        gated0 = pool.tile([P, half], F32, name="gated0", tag="turn", align_bytes=64)
-        quantize(joint_codes, joint_scales, joint[:])
-        for h in range(2):
-            cols = slice(N + h * part, N + (h + 1) * part)
-            product(acc0[h], joint_codes[:, cols], joint_scales[:, cols])
-            relu_gate(gated0[:, parts[h]], acc0[h], gate_sb[:, parts[h]])
-        for h in range(2):
-            entries = offsets[:, h * part // 16 : (h + 1) * part // 16]
-            nc.vector.tensor_tensor(new[:, parts[h]], window[:].indirect(entries), gated0[:, parts[h]], ALU.add)
-        scalar_gather(old[:], window[:].indirect(lists[1]))
-        codes1 = pool.tile([P, half], U32, name="codes1", tag="turn", align_bytes=64)
-        scales1 = pool.tile([P, half], U8, name="scales1", align_bytes=64)
-        acc1 = psum.tile([P, half], F32, name="acc1")
-        gated = pool.tile([P, half], F32, name="gated")
-        quantize(codes1, scales1, picked[1])
-        product(acc1, codes1[:], scales1[:])
-        relu_gate(gated[:], acc1, gate_sb[:, span[1]])
-        nc.scalar.activation(window[:].indirect(lists[0]), new[:], ACT.Copy)
-        nc.vector.tensor_tensor(window[:].indirect(lists[1]), old[:], gated[:], ALU.add)
+        gated = pool.tile([P, S], F32, name="gated")
+        old = pool.tile([P, S], F32, name="old")
+        rectified = pool.tile([P, part], F32, name="rectified")
+        nc.scalar.activation(rectified[:], acc[0][:], ACT.Relu)
+        nc.gpsimd.tensor_tensor(gated[:, 0:part], rectified[:], gate_sb[:, 0:part], ALU.mult)
+        nc.vector.tensor_copy(old[:, 0:half], window[:].indirect(entries(0, half)))
+        scalar_gather(old[:, half:S], window[:].indirect(entries(half, S)))
+        nc.vector.scalar_tensor_tensor(gated[:, part:S], acc[1][:], 0.0, gate_sb[:, part:S], ALU.max, ALU.mult)
+        nc.vector.tensor_tensor(window[:].indirect(offsets[:]), old[:], gated[:], ALU.add)
         nc.sync.dma_start(out, window[:])

@@ -32,11 +32,11 @@ def tile_picked_modres_linrelu_l_kernel(tc, xT, gate, res, w1, offs, out):
         window = pool.tile([P, T], F32, name="window")
 
         x_rows = xT.rearrange("(p j) t -> p j t", j=PACK)
+        nc.sync.dma_start(w_raw[:], w1.rearrange("(p j) m -> p j m", j=PACK))
         nc.sync.dma_start(first[:], x_rows[:, 0:2, :])
         nc.sync.dma_start(offsets[:], offs)
         nc.sync.dma_start(later[0][:], x_rows[:, 2, :])
         nc.sync.dma_start(later[1][:], x_rows[:, 3, :])
-        nc.sync.dma_start(w_raw[:], w1.rearrange("(p j) m -> p j m", j=PACK))
         nc.sync.dma_start(window[:], res)
         nc.sync.dma_start(gate_sb[:], gate)
 
@@ -61,6 +61,8 @@ def tile_picked_modres_linrelu_l_kernel(tc, xT, gate, res, w1, offs, out):
         def scalar_gather(dst, src):
             nc.scalar.activation(dst, src, ACT.Copy)
 
+        nc.scalar.copy(w_grouped[:], w_raw[:].rearrange("p j m -> p m j"))
+        quantize(w_codes, w_scales, w_grouped[:])
         early = pool.tile([P, 2, S], F32, name="early")
         late = [pool.tile([P, 2, part], BF16, name=f"late{h}") for h in range(2)]
         for j in range(2):
@@ -74,8 +76,6 @@ def tile_picked_modres_linrelu_l_kernel(tc, xT, gate, res, w1, offs, out):
                 scalar_gather(late[h][:, j, :], later[j][:].indirect(entries(half + h * part, half + (h + 1) * part)))
         for h in range(2):
             nc.scalar.copy(laid[h][:, :, 2:4], late[h][:].rearrange("p e s -> p s e"))
-        nc.gpsimd.tensor_scalar(w_grouped[:], w_raw[:].rearrange("p j m -> p m j"), 1.0, 0.0, ALU.mult, ALU.add)
-        quantize(w_codes, w_scales, w_grouped[:])
         grouped = [stepped[:, span[0], :], stepped[:, span[1], :], laid[0][:], laid[1][:]]
         for h in range(4):
             quantize(codes[h], scales[h], grouped[h])

@@ -16,6 +16,7 @@ ACT = mybir.ActivationFunctionType
 
 P = 128
 PACK = 4
+RES_ON_VECTOR = 192
 
 
 def tile_picked_modres_linrelu_l_kernel(tc, xT, gate, res, w1, offs, out):
@@ -97,8 +98,8 @@ def tile_picked_modres_linrelu_l_kernel(tc, xT, gate, res, w1, offs, out):
         rectified = pool.tile([P, part], F32, name="rectified")
         nc.scalar.activation(rectified[:], acc[0][:], ACT.Relu)
         nc.gpsimd.tensor_tensor(gated[:, 0:part], rectified[:], gate_sb[:, 0:part], ALU.mult)
-        nc.vector.tensor_copy(old[:, 0:half], window[:].indirect(entries(0, half)))
-        scalar_gather(old[:, half:S], window[:].indirect(entries(half, S)))
+        nc.vector.tensor_copy(old[:, 0:RES_ON_VECTOR], window[:].indirect(entries(0, RES_ON_VECTOR)))
+        scalar_gather(old[:, RES_ON_VECTOR:S], window[:].indirect(entries(RES_ON_VECTOR, S)))
         nc.vector.scalar_tensor_tensor(gated[:, part:S], acc[1][:], 0.0, gate_sb[:, part:S], ALU.max, ALU.mult)
         nc.vector.tensor_tensor(window[:].indirect(offsets[:]), old[:], gated[:], ALU.add)
         nc.sync.dma_start(out, window[:])

@@ -1,6 +1,7 @@
 from contextlib import ExitStack
 
 import concourse.mybir as mybir
+from concourse.masks import make_identity
 
 K, T, S, N = 512, 2048, 512, 128
 FLOPS = 2 * K * S * N
@@ -16,7 +17,9 @@ ACT = mybir.ActivationFunctionType
 
 P = 128
 PACK = 4
-RES_ON_VECTOR = 192
+HALF = S // 2
+PIECE = S // 4
+LEAD = 128
 
 
 def tile_picked_modres_linrelu_l_kernel(tc, xT, gate, res, w1, offs, out):
@@ -29,77 +32,89 @@ def tile_picked_modres_linrelu_l_kernel(tc, xT, gate, res, w1, offs, out):
         first = pool.tile([P, 2, T], F32, name="first")
         later = [pool.tile([P, T], F32, name=f"later{j}") for j in range(2)]
         w_raw = pool.tile([P, PACK, N], F32, name="w_raw")
-        gate_sb = pool.tile([P, S], F32, name="gate_sb")
-        window = pool.tile([P, T], F32, name="window")
+        gate_cols = pool.tile([P, 4], F32, name="gate_cols")
+        identity = pool.tile([P, P], F32, name="identity")
+        early_rows = pool.tile([P, T], F32, name="early_rows")
+        late_rows = pool.tile([P, T], F32, name="late_rows")
+
+        make_identity(nc, identity[:])
+        nc.vector.memset(early_rows[:], 0.0)
+        nc.vector.memset(late_rows[:], 0.0)
 
         x_rows = xT.rearrange("(p j) t -> p j t", j=PACK)
         nc.sync.dma_start(w_raw[:], w1.rearrange("(p j) m -> p j m", j=PACK))
+        nc.sync.dma_start(gate_cols[:], gate[0, :].rearrange("(p i) -> p i", i=4))
         nc.sync.dma_start(first[:], x_rows[:, 0:2, :])
         nc.sync.dma_start(offsets[:], offs)
         nc.sync.dma_start(later[0][:], x_rows[:, 2, :])
         nc.sync.dma_start(later[1][:], x_rows[:, 3, :])
-        nc.sync.dma_start(window[:], res)
-        nc.sync.dma_start(gate_sb[:], gate)
-
-        half = S // 2
-        part = half // 2
+        nc.sync.dma_start(early_rows[0:P:2, :], res[0:N:2, :])
+        nc.sync.dma_start(late_rows[1:P:2, :], res[1:N:2, :])
 
         def entries(lo, hi):
             return offsets[:, lo // 16 : hi // 16]
 
-        stepped = pool.tile([P, half, PACK], BF16, name="stepped", align_bytes=64)
-        laid = [pool.tile([P, part, PACK], BF16, name=f"laid{h}", align_bytes=64) for h in range(2)]
-        codes = [pool.tile([P, part], U32, name=f"codes{h}", align_bytes=64) for h in range(4)]
-        scales = [pool.tile([P, part], U8, name=f"scales{h}", align_bytes=64) for h in range(4)]
+        halves = [slice(h * HALF, (h + 1) * HALF) for h in range(2)]
+
+        spread = psum.tile([P, 4, P], F32, name="spread")
+        for i in range(4):
+            nc.tensor.transpose(spread[:, i, :], gate_cols[:, i : i + 1].to_broadcast([P, P]), identity[:])
+        gate_sb = pool.tile([P, S], F32, name="gate_sb")
+        nc.scalar.copy(gate_sb[:].rearrange("p (c i) -> p c i", i=4), spread[:].rearrange("p i c -> p c i"))
+
+        grouped = [pool.tile([P, HALF, PACK], BF16, name=f"grouped{h}", align_bytes=64) for h in range(2)]
+        spans = [(0, PIECE), (PIECE, HALF), (HALF, S)]
+        codes = [pool.tile([P, hi - lo], U32, name=f"codes{lo}", align_bytes=64) for lo, hi in spans]
+        scales = [pool.tile([P, hi - lo], U8, name=f"scales{lo}", align_bytes=64) for lo, hi in spans]
         w_grouped = pool.tile([P, N, PACK], BF16, name="w_grouped", align_bytes=64)
         w_codes = pool.tile([P, N], U32, name="w_codes", align_bytes=64)
         w_scales = pool.tile([P, N], U8, name="w_scales", align_bytes=64)
-        span = [slice(h * part, (h + 1) * part) for h in range(4)]
 
         def quantize(codes, scales, grouped):
             nc.vector.quantize_mx(out=codes[:].bitcast(FP8X4), scales=scales[:], in_=grouped.rearrange("p s j -> p (s j)"))
 
-        def scalar_gather(dst, src):
-            nc.scalar.activation(dst, src, ACT.Copy)
-
         nc.scalar.copy(w_grouped[:], w_raw[:].rearrange("p j m -> p m j"))
         quantize(w_codes, w_scales, w_grouped[:])
-        early = pool.tile([P, 2, S], F32, name="early")
-        late = [pool.tile([P, 2, part], BF16, name=f"late{h}") for h in range(2)]
-        for j in range(2):
-            nc.vector.tensor_copy(early[:, j, :], first[:, j, :].indirect(offsets[:]))
-        nc.vector.tensor_copy(stepped[:, :, 0:2], early[:, :, 0:half].rearrange("p e s -> p s e"))
-        for h in range(2):
-            nc.scalar.copy(laid[h][:, :, 0:2], early[:, :, span[2 + h]].rearrange("p e s -> p s e"))
-        for j in range(2):
-            nc.vector.tensor_copy(stepped[:, :, 2 + j], later[j][:].indirect(entries(0, half)))
-            for h in range(2):
-                scalar_gather(late[h][:, j, :], later[j][:].indirect(entries(half + h * part, half + (h + 1) * part)))
-        for h in range(2):
-            nc.scalar.copy(laid[h][:, :, 2:4], late[h][:].rearrange("p e s -> p s e"))
-        grouped = [stepped[:, span[0], :], stepped[:, span[1], :], laid[0][:], laid[1][:]]
-        for h in range(4):
-            quantize(codes[h], scales[h], grouped[h])
 
-        acc = [psum.tile([P, part], F32, name="acc0"), psum.tile([P, S - part], F32, name="acc1")]
-        outs = [acc[0][:]] + [acc[1][:, span[h]] for h in range(3)]
-        for h in range(4):
+        staged = pool.tile([P, 2, HALF], F32, name="staged")
+        for j in range(2):
+            nc.vector.tensor_copy(grouped[0][:, :, j], first[:, j, :].indirect(entries(0, HALF)))
+            nc.scalar.activation(staged[:, j, :], first[:, j, :].indirect(entries(HALF, S)), ACT.Copy)
+        nc.scalar.copy(grouped[1][:, :, 0:2], staged[:].rearrange("p e s -> p s e"))
+        for j in range(2):
+            nc.vector.tensor_copy(grouped[0][:, :, 2 + j], later[j][:].indirect(entries(0, HALF)))
+            nc.scalar.activation(grouped[1][:, :, 2 + j], later[j][:].indirect(entries(HALF, S)), ACT.Copy)
+
+        acc = [psum.tile([P, HALF], F32, name=f"acc{h}") for h in range(2)]
+        gated_first = pool.tile([P, HALF], F32, name="gated_first")
+        mixed = pool.tile([P, S], F32, name="mixed")
+        late_sum = pool.tile([P, HALF], F32, name="late_sum")
+        old_early = pool.tile([P, S], F32, name="old_early")
+        old_late = pool.tile([P, S], F32, name="old_late")
+        for q, (lo, hi) in enumerate(spans):
+            quantize(codes[q], scales[q], grouped[lo // HALF][:, lo % HALF : lo % HALF + hi - lo, :])
+        for q, (lo, hi) in enumerate(spans):
             nc.tensor.matmul_mx(
-                out=outs[h],
+                out=acc[lo // HALF][:, lo % HALF : lo % HALF + hi - lo],
                 lhsT=w_codes[:].bitcast(FP8X4),
                 lhsT_scale=w_scales[:],
-                rhs=codes[h][:].bitcast(FP8X4),
-                rhs_scale=scales[h][:],
+                rhs=codes[q][:].bitcast(FP8X4),
+                rhs_scale=scales[q][:],
                 start=True,
                 stop=True,
             )
-        gated = pool.tile([P, S], F32, name="gated")
-        old = pool.tile([P, S], F32, name="old")
-        rectified = pool.tile([P, part], F32, name="rectified")
-        nc.scalar.activation(rectified[:], acc[0][:], ACT.Relu)
-        nc.gpsimd.tensor_tensor(gated[:, 0:part], rectified[:], gate_sb[:, 0:part], ALU.mult)
-        nc.vector.tensor_copy(old[:, 0:RES_ON_VECTOR], window[:].indirect(entries(0, RES_ON_VECTOR)))
-        scalar_gather(old[:, RES_ON_VECTOR:S], window[:].indirect(entries(RES_ON_VECTOR, S)))
-        nc.vector.scalar_tensor_tensor(gated[:, part:S], acc[1][:], 0.0, gate_sb[:, part:S], ALU.max, ALU.mult)
-        nc.vector.tensor_tensor(window[:].indirect(offsets[:]), old[:], gated[:], ALU.add)
-        nc.sync.dma_start(out, window[:])
+        nc.scalar.activation(old_early[:], early_rows[:].indirect(offsets[:]), ACT.Copy)
+        gated = [gated_first[:], mixed[:, halves[1]]]
+        for h in range(2):
+            nc.vector.scalar_tensor_tensor(gated[h], acc[h][:], 0.0, gate_sb[:, halves[h]], ALU.max, ALU.mult)
+        for h in range(2):
+            nc.scalar.activation(old_late[:, halves[h]], late_rows[:].indirect(entries(h * HALF, (h + 1) * HALF)), ACT.Copy)
+        nc.vector.tensor_tensor(early_rows[:].indirect(entries(0, LEAD)), old_early[:, 0:LEAD], gated_first[:, 0:LEAD], ALU.add)
+        summed = [mixed[:, halves[0]], late_sum[:]]
+        for h in range(2):
+            nc.vector.tensor_tensor(summed[h], old_late[:, halves[h]], gated[h], ALU.add)
+        nc.vector.tensor_tensor(early_rows[:].indirect(entries(LEAD, S)), old_early[:, LEAD:S], mixed[:, LEAD:S], ALU.add)
+        for h in range(2):
+            nc.scalar.activation(late_rows[:].indirect(entries(h * HALF, (h + 1) * HALF)), summed[h], ACT.Copy)
+        nc.sync.dma_start(out[0:N:2, :], early_rows[0:P:2, :])
+        nc.sync.dma_start(out[1:N:2, :], late_rows[1:P:2, :])

@@ -19,7 +19,7 @@ P = 128
 PACK = 4
 HALF = S // 2
 PIECE = S // 4
-LEAD = 128
+RES_ON_VECTOR = 160
 
 
 def tile_picked_modres_linrelu_l_kernel(tc, xT, gate, res, w1, offs, out):
@@ -29,32 +29,26 @@ def tile_picked_modres_linrelu_l_kernel(tc, xT, gate, res, w1, offs, out):
         psum = ctx.enter_context(tc.psum_pool(name="psum", bufs=1))
 
         offsets = pool.tile([P, S // 16], U16, name="offsets")
-        first = pool.tile([P, 2, T], F32, name="first")
-        later = [pool.tile([P, T], F32, name=f"later{j}") for j in range(2)]
-        w_raw = pool.tile([P, PACK, N], F32, name="w_raw")
+        first = pool.tile([P, 2, T], F32, name="first", align_bytes=256)
+        later = [pool.tile([P, T], F32, name=f"later{j}", align_bytes=256) for j in range(2)]
+        w_raw = pool.tile([P, PACK, N], F32, name="w_raw", tag="w_raw", align_bytes=256)
         gate_cols = pool.tile([P, 4], F32, name="gate_cols")
-        identity = pool.tile([P, P], F32, name="identity")
-        early_rows = pool.tile([P, T], F32, name="early_rows")
-        late_rows = pool.tile([P, T], F32, name="late_rows")
+        identity = pool.tile([P, P], F32, name="identity", tag="identity")
+        window = pool.tile([P, T], F32, name="window", align_bytes=256)
 
         make_identity(nc, identity[:])
-        nc.vector.memset(early_rows[:], 0.0)
-        nc.vector.memset(late_rows[:], 0.0)
 
         x_rows = xT.rearrange("(p j) t -> p j t", j=PACK)
-        nc.sync.dma_start(w_raw[:], w1.rearrange("(p j) m -> p j m", j=PACK))
         nc.sync.dma_start(gate_cols[:], gate[0, :].rearrange("(p i) -> p i", i=4))
         nc.sync.dma_start(first[:], x_rows[:, 0:2, :])
         nc.sync.dma_start(offsets[:], offs)
         nc.sync.dma_start(later[0][:], x_rows[:, 2, :])
         nc.sync.dma_start(later[1][:], x_rows[:, 3, :])
-        nc.sync.dma_start(early_rows[0:P:2, :], res[0:N:2, :])
-        nc.sync.dma_start(late_rows[1:P:2, :], res[1:N:2, :])
+        nc.sync.dma_start(w_raw[:], w1.rearrange("(p j) m -> p j m", j=PACK))
+        nc.sync.dma_start(window[:], res)
 
         def entries(lo, hi):
             return offsets[:, lo // 16 : hi // 16]
-
-        halves = [slice(h * HALF, (h + 1) * HALF) for h in range(2)]
 
         spread = psum.tile([P, 4, P], F32, name="spread")
         for i in range(4):
@@ -63,20 +57,16 @@ def tile_picked_modres_linrelu_l_kernel(tc, xT, gate, res, w1, offs, out):
         nc.scalar.copy(gate_sb[:].rearrange("p (c i) -> p c i", i=4), spread[:].rearrange("p i c -> p c i"))
 
         grouped = [pool.tile([P, HALF, PACK], BF16, name=f"grouped{h}", align_bytes=64) for h in range(2)]
-        spans = [(0, PIECE), (PIECE, HALF), (HALF, S)]
-        codes = [pool.tile([P, hi - lo], U32, name=f"codes{lo}", align_bytes=64) for lo, hi in spans]
+        spans = [(q * PIECE, (q + 1) * PIECE) for q in range(4)]
         scales = [pool.tile([P, hi - lo], U8, name=f"scales{lo}", align_bytes=64) for lo, hi in spans]
-        w_grouped = pool.tile([P, N, PACK], BF16, name="w_grouped", align_bytes=64)
+        w_grouped = [pool.tile([P, N // 2, PACK], BF16, name=f"w_grouped{h}", align_bytes=64) for h in range(2)]
         w_codes = pool.tile([P, N], U32, name="w_codes", align_bytes=64)
         w_scales = pool.tile([P, N], U8, name="w_scales", align_bytes=64)
 
         def quantize(codes, scales, grouped):
-            nc.vector.quantize_mx(out=codes[:].bitcast(FP8X4), scales=scales[:], in_=grouped.rearrange("p s j -> p (s j)"))
+            nc.vector.quantize_mx(out=codes.bitcast(FP8X4), scales=scales, in_=grouped.rearrange("p s j -> p (s j)"))
 
-        nc.scalar.copy(w_grouped[:], w_raw[:].rearrange("p j m -> p m j"))
-        quantize(w_codes, w_scales, w_grouped[:])
-
-        staged = pool.tile([P, 2, HALF], F32, name="staged")
+        staged = pool.tile([P, 2, HALF], F32, name="staged", tag="identity")
         for j in range(2):
             nc.vector.tensor_copy(grouped[0][:, :, j], first[:, j, :].indirect(entries(0, HALF)))
             nc.scalar.activation(staged[:, j, :], first[:, j, :].indirect(entries(HALF, S)), ACT.Copy)
@@ -85,36 +75,34 @@ def tile_picked_modres_linrelu_l_kernel(tc, xT, gate, res, w1, offs, out):
             nc.vector.tensor_copy(grouped[0][:, :, 2 + j], later[j][:].indirect(entries(0, HALF)))
             nc.scalar.activation(grouped[1][:, :, 2 + j], later[j][:].indirect(entries(HALF, S)), ACT.Copy)
 
-        acc = [psum.tile([P, HALF], F32, name=f"acc{h}") for h in range(2)]
-        gated_first = pool.tile([P, HALF], F32, name="gated_first")
-        mixed = pool.tile([P, S], F32, name="mixed")
-        late_sum = pool.tile([P, HALF], F32, name="late_sum")
-        old_early = pool.tile([P, S], F32, name="old_early")
-        old_late = pool.tile([P, S], F32, name="old_late")
-        for q, (lo, hi) in enumerate(spans):
-            quantize(codes[q], scales[q], grouped[lo // HALF][:, lo % HALF : lo % HALF + hi - lo, :])
+        acc = [psum.tile([P, PIECE], F32, name=f"acc{q}") for q in range(4)]
+        gated = pool.tile([P, S], F32, name="gated")
+        old = pool.tile([P, S], F32, name="old")
+        w_cols = [slice(h * N // 2, (h + 1) * N // 2) for h in range(2)]
+        nc.gpsimd.tensor_copy(w_grouped[0][:], w_raw[:, :, w_cols[0]].rearrange("p j m -> p m j"))
+        nc.scalar.copy(w_grouped[1][:], w_raw[:, :, w_cols[1]].rearrange("p j m -> p m j"))
+        first_codes = pool.tile([P, HALF], U32, name="first_codes", align_bytes=64)
+        for q in range(2):
+            quantize(first_codes[:, slice(*spans[q])], scales[q][:], grouped[0][:, slice(*spans[q]), :])
+        for h in range(2):
+            quantize(w_codes[:, w_cols[h]], w_scales[:, w_cols[h]], w_grouped[h][:])
+        second_codes = pool.tile([P, HALF], U32, name="second_codes", tag="w_raw", align_bytes=256)
+        for q in range(2):
+            quantize(second_codes[:, slice(*spans[q])], scales[2 + q][:], grouped[1][:, slice(*spans[q]), :])
+        codes = [half_codes[:, slice(*spans[q])] for half_codes in (first_codes, second_codes) for q in range(2)]
         for q, (lo, hi) in enumerate(spans):
             nc.tensor.matmul_mx(
-                out=acc[lo // HALF][:, lo % HALF : lo % HALF + hi - lo],
+                out=acc[q][:],
                 lhsT=w_codes[:].bitcast(FP8X4),
                 lhsT_scale=w_scales[:],
-                rhs=codes[q][:].bitcast(FP8X4),
+                rhs=codes[q].bitcast(FP8X4),
                 rhs_scale=scales[q][:],
                 start=True,
                 stop=True,
             )
-        nc.scalar.activation(old_early[:], early_rows[:].indirect(offsets[:]), ACT.Copy)
-        gated = [gated_first[:], mixed[:, halves[1]]]
-        for h in range(2):
-            nc.vector.scalar_tensor_tensor(gated[h], acc[h][:], 0.0, gate_sb[:, halves[h]], ALU.max, ALU.mult)
-        for h in range(2):
-            nc.scalar.activation(old_late[:, halves[h]], late_rows[:].indirect(entries(h * HALF, (h + 1) * HALF)), ACT.Copy)
-        nc.vector.tensor_tensor(early_rows[:].indirect(entries(0, LEAD)), old_early[:, 0:LEAD], gated_first[:, 0:LEAD], ALU.add)
-        summed = [mixed[:, halves[0]], late_sum[:]]
-        for h in range(2):
-            nc.vector.tensor_tensor(summed[h], old_late[:, halves[h]], gated[h], ALU.add)
-        nc.vector.tensor_tensor(early_rows[:].indirect(entries(LEAD, S)), old_early[:, LEAD:S], mixed[:, LEAD:S], ALU.add)
-        for h in range(2):
-            nc.scalar.activation(late_rows[:].indirect(entries(h * HALF, (h + 1) * HALF)), summed[h], ACT.Copy)
-        nc.sync.dma_start(out[0:N:2, :], early_rows[0:P:2, :])
-        nc.sync.dma_start(out[1:N:2, :], late_rows[1:P:2, :])
+        for q, (lo, hi) in enumerate(spans):
+            nc.vector.scalar_tensor_tensor(gated[:, lo:hi], acc[q][:], 0.0, gate_sb[:, lo:hi], ALU.max, ALU.mult)
+        nc.vector.tensor_copy(old[:, 0:RES_ON_VECTOR], window[:].indirect(entries(0, RES_ON_VECTOR)))
+        nc.scalar.activation(old[:, RES_ON_VECTOR:S], window[:].indirect(entries(RES_ON_VECTOR, S)), ACT.Copy)
+        nc.vector.tensor_tensor(window[:].indirect(offsets[:]), old[:], gated[:], ALU.add)
+        nc.sync.dma_start(out, window[:])

@@ -19,7 +19,8 @@ P = 128
 PACK = 4
 HALF = S // 2
 PIECE = S // 4
-RES_ON_VECTOR = 160
+X_ON_SCALAR = 192
+RES_ON_VECTOR = 224
 
 
 def tile_picked_modres_linrelu_l_kernel(tc, xT, gate, res, w1, offs, out):
@@ -39,8 +40,8 @@ def tile_picked_modres_linrelu_l_kernel(tc, xT, gate, res, w1, offs, out):
         make_identity(nc, identity[:])
 
         x_rows = xT.rearrange("(p j) t -> p j t", j=PACK)
-        nc.sync.dma_start(gate_cols[:], gate[0, :].rearrange("(p i) -> p i", i=4))
         nc.sync.dma_start(first[:], x_rows[:, 0:2, :])
+        nc.sync.dma_start(gate_cols[:], gate[0, :].rearrange("(p i) -> p i", i=4))
         nc.sync.dma_start(offsets[:], offs)
         nc.sync.dma_start(later[0][:], x_rows[:, 2, :])
         nc.sync.dma_start(later[1][:], x_rows[:, 3, :])
@@ -56,7 +57,7 @@ def tile_picked_modres_linrelu_l_kernel(tc, xT, gate, res, w1, offs, out):
         gate_sb = pool.tile([P, S], F32, name="gate_sb")
         nc.scalar.copy(gate_sb[:].rearrange("p (c i) -> p c i", i=4), spread[:].rearrange("p i c -> p c i"))
 
-        grouped = [pool.tile([P, HALF, PACK], BF16, name=f"grouped{h}", align_bytes=64) for h in range(2)]
+        grouped = pool.tile([P, S, PACK], BF16, name="grouped", align_bytes=64)
         spans = [(q * PIECE, (q + 1) * PIECE) for q in range(4)]
         scales = [pool.tile([P, hi - lo], U8, name=f"scales{lo}", align_bytes=64) for lo, hi in spans]
         w_grouped = [pool.tile([P, N // 2, PACK], BF16, name=f"w_grouped{h}", align_bytes=64) for h in range(2)]
@@ -66,14 +67,14 @@ def tile_picked_modres_linrelu_l_kernel(tc, xT, gate, res, w1, offs, out):
         def quantize(codes, scales, grouped):
             nc.vector.quantize_mx(out=codes.bitcast(FP8X4), scales=scales, in_=grouped.rearrange("p s j -> p (s j)"))
 
-        staged = pool.tile([P, 2, HALF], F32, name="staged", tag="identity")
+        staged = pool.tile([P, 2, X_ON_SCALAR], F32, name="staged", tag="identity")
         for j in range(2):
-            nc.vector.tensor_copy(grouped[0][:, :, j], first[:, j, :].indirect(entries(0, HALF)))
-            nc.scalar.activation(staged[:, j, :], first[:, j, :].indirect(entries(HALF, S)), ACT.Copy)
-        nc.scalar.copy(grouped[1][:, :, 0:2], staged[:].rearrange("p e s -> p s e"))
+            nc.vector.tensor_copy(grouped[:, X_ON_SCALAR:S, j], first[:, j, :].indirect(entries(X_ON_SCALAR, S)))
+            nc.scalar.activation(staged[:, j, :], first[:, j, :].indirect(entries(0, X_ON_SCALAR)), ACT.Copy)
+        nc.scalar.copy(grouped[:, 0:X_ON_SCALAR, 0:2], staged[:].rearrange("p e s -> p s e"))
         for j in range(2):
-            nc.vector.tensor_copy(grouped[0][:, :, 2 + j], later[j][:].indirect(entries(0, HALF)))
-            nc.scalar.activation(grouped[1][:, :, 2 + j], later[j][:].indirect(entries(HALF, S)), ACT.Copy)
+            nc.vector.tensor_copy(grouped[:, X_ON_SCALAR:S, 2 + j], later[j][:].indirect(entries(X_ON_SCALAR, S)))
+            nc.scalar.activation(grouped[:, 0:X_ON_SCALAR, 2 + j], later[j][:].indirect(entries(0, X_ON_SCALAR)), ACT.Copy)
 
         acc = [psum.tile([P, PIECE], F32, name=f"acc{q}") for q in range(4)]
         gated = pool.tile([P, S], F32, name="gated")
@@ -81,15 +82,14 @@ def tile_picked_modres_linrelu_l_kernel(tc, xT, gate, res, w1, offs, out):
         w_cols = [slice(h * N // 2, (h + 1) * N // 2) for h in range(2)]
         nc.gpsimd.tensor_copy(w_grouped[0][:], w_raw[:, :, w_cols[0]].rearrange("p j m -> p m j"))
         nc.scalar.copy(w_grouped[1][:], w_raw[:, :, w_cols[1]].rearrange("p j m -> p m j"))
-        first_codes = pool.tile([P, HALF], U32, name="first_codes", align_bytes=64)
-        for q in range(2):
-            quantize(first_codes[:, slice(*spans[q])], scales[q][:], grouped[0][:, slice(*spans[q]), :])
+        first_codes = pool.tile([P, PIECE], U32, name="first_codes", align_bytes=64)
+        quantize(first_codes[:], scales[0][:], grouped[:, 0:PIECE, :])
         for h in range(2):
             quantize(w_codes[:, w_cols[h]], w_scales[:, w_cols[h]], w_grouped[h][:])
-        second_codes = pool.tile([P, HALF], U32, name="second_codes", tag="w_raw", align_bytes=256)
-        for q in range(2):
-            quantize(second_codes[:, slice(*spans[q])], scales[2 + q][:], grouped[1][:, slice(*spans[q]), :])
-        codes = [half_codes[:, slice(*spans[q])] for half_codes in (first_codes, second_codes) for q in range(2)]
+        rest_codes = pool.tile([P, S - PIECE], U32, name="rest_codes", tag="w_raw", align_bytes=256)
+        codes = [first_codes[:]] + [rest_codes[:, slice(*spans[q])] for q in range(3)]
+        for q in range(1, 4):
+            quantize(codes[q], scales[q][:], grouped[:, slice(*spans[q]), :])
         for q, (lo, hi) in enumerate(spans):
             nc.tensor.matmul_mx(
                 out=acc[q][:],

from contextlib import ExitStack

import concourse.mybir as mybir
from concourse.masks import make_identity

K, T, S, N = 512, 2048, 512, 128
FLOPS = 2 * K * S * N

F32 = mybir.dt.float32
BF16 = mybir.dt.bfloat16
U32 = mybir.dt.uint32
U16 = mybir.dt.uint16
U8 = mybir.dt.uint8
FP8X4 = mybir.dt.float8_e4m3fn_x4
ALU = mybir.AluOpType
ACT = mybir.ActivationFunctionType

P = 128
PACK = 4
HALF = S // 2
PIECE = S // 4
X_ON_SCALAR = 192
RES_ON_VECTOR = 224


def tile_picked_modres_linrelu_l_kernel(tc, xT, gate, res, w1, offs, out):
    nc = tc.nc
    with ExitStack() as ctx:
        pool = ctx.enter_context(tc.tile_pool(name="held", bufs=1))
        psum = ctx.enter_context(tc.psum_pool(name="psum", bufs=1))

        offsets = pool.tile([P, S // 16], U16, name="offsets")
        first = pool.tile([P, 2, T], F32, name="first", align_bytes=256)
        later = [pool.tile([P, T], F32, name=f"later{j}", align_bytes=256) for j in range(2)]
        w_raw = pool.tile([P, PACK, N], F32, name="w_raw", tag="w_raw", align_bytes=256)
        gate_cols = pool.tile([P, 4], F32, name="gate_cols")
        identity = pool.tile([P, P], F32, name="identity", tag="identity")
        window = pool.tile([P, T], F32, name="window", align_bytes=256)

        make_identity(nc, identity[:])

        x_rows = xT.rearrange("(p j) t -> p j t", j=PACK)
        nc.sync.dma_start(first[:], x_rows[:, 0:2, :])
        nc.sync.dma_start(gate_cols[:], gate[0, :].rearrange("(p i) -> p i", i=4))
        nc.sync.dma_start(offsets[:], offs)
        nc.sync.dma_start(later[0][:], x_rows[:, 2, :])
        nc.sync.dma_start(later[1][:], x_rows[:, 3, :])
        nc.sync.dma_start(w_raw[:], w1.rearrange("(p j) m -> p j m", j=PACK))
        nc.sync.dma_start(window[:], res)

        def entries(lo, hi):
            return offsets[:, lo // 16 : hi // 16]

        spread = psum.tile([P, 4, P], F32, name="spread")
        for i in range(4):
            nc.tensor.transpose(spread[:, i, :], gate_cols[:, i : i + 1].to_broadcast([P, P]), identity[:])
        gate_sb = pool.tile([P, S], F32, name="gate_sb")
        nc.scalar.copy(gate_sb[:].rearrange("p (c i) -> p c i", i=4), spread[:].rearrange("p i c -> p c i"))

        grouped = pool.tile([P, S, PACK], BF16, name="grouped", align_bytes=64)
        spans = [(q * PIECE, (q + 1) * PIECE) for q in range(4)]
        scales = [pool.tile([P, hi - lo], U8, name=f"scales{lo}", align_bytes=64) for lo, hi in spans]
        w_grouped = [pool.tile([P, N // 2, PACK], BF16, name=f"w_grouped{h}", align_bytes=64) for h in range(2)]
        w_codes = pool.tile([P, N], U32, name="w_codes", align_bytes=64)
        w_scales = pool.tile([P, N], U8, name="w_scales", align_bytes=64)

        def quantize(codes, scales, grouped):
            nc.vector.quantize_mx(out=codes.bitcast(FP8X4), scales=scales, in_=grouped.rearrange("p s j -> p (s j)"))

        staged = pool.tile([P, 2, X_ON_SCALAR], F32, name="staged", tag="identity")
        for j in range(2):
            nc.vector.tensor_copy(grouped[:, X_ON_SCALAR:S, j], first[:, j, :].indirect(entries(X_ON_SCALAR, S)))
            nc.scalar.activation(staged[:, j, :], first[:, j, :].indirect(entries(0, X_ON_SCALAR)), ACT.Copy)
        nc.scalar.copy(grouped[:, 0:X_ON_SCALAR, 0:2], staged[:].rearrange("p e s -> p s e"))
        for j in range(2):
            nc.vector.tensor_copy(grouped[:, X_ON_SCALAR:S, 2 + j], later[j][:].indirect(entries(X_ON_SCALAR, S)))
            nc.scalar.activation(grouped[:, 0:X_ON_SCALAR, 2 + j], later[j][:].indirect(entries(0, X_ON_SCALAR)), ACT.Copy)

        acc = [psum.tile([P, PIECE], F32, name=f"acc{q}") for q in range(4)]
        gated = pool.tile([P, S], F32, name="gated")
        old = pool.tile([P, S], F32, name="old")
        w_cols = [slice(h * N // 2, (h + 1) * N // 2) for h in range(2)]
        nc.gpsimd.tensor_copy(w_grouped[0][:], w_raw[:, :, w_cols[0]].rearrange("p j m -> p m j"))
        nc.scalar.copy(w_grouped[1][:], w_raw[:, :, w_cols[1]].rearrange("p j m -> p m j"))
        first_codes = pool.tile([P, PIECE], U32, name="first_codes", align_bytes=64)
        quantize(first_codes[:], scales[0][:], grouped[:, 0:PIECE, :])
        for h in range(2):
            quantize(w_codes[:, w_cols[h]], w_scales[:, w_cols[h]], w_grouped[h][:])
        rest_codes = pool.tile([P, S - PIECE], U32, name="rest_codes", tag="w_raw", align_bytes=256)
        codes = [first_codes[:]] + [rest_codes[:, slice(*spans[q])] for q in range(3)]
        for q in range(1, 4):
            quantize(codes[q], scales[q][:], grouped[:, slice(*spans[q]), :])
        for q, (lo, hi) in enumerate(spans):
            nc.tensor.matmul_mx(
                out=acc[q][:],
                lhsT=w_codes[:].bitcast(FP8X4),
                lhsT_scale=w_scales[:],
                rhs=codes[q].bitcast(FP8X4),
                rhs_scale=scales[q][:],
                start=True,
                stop=True,
            )
        for q, (lo, hi) in enumerate(spans):
            nc.vector.scalar_tensor_tensor(gated[:, lo:hi], acc[q][:], 0.0, gate_sb[:, lo:hi], ALU.max, ALU.mult)
        nc.vector.tensor_copy(old[:, 0:RES_ON_VECTOR], window[:].indirect(entries(0, RES_ON_VECTOR)))
        nc.scalar.activation(old[:, RES_ON_VECTOR:S], window[:].indirect(entries(RES_ON_VECTOR, S)), ACT.Copy)
        nc.vector.tensor_tensor(window[:].indirect(offsets[:]), old[:], gated[:], ALU.add)
        nc.sync.dma_start(out, window[:])
